import numpy as np, ml_dtypes
CORES = [19,27,51,107,147,155,179,235,275,283,307,363,403,411,435,491]
N = 16
GR, GC, TK = 8, 2, 512
RA = [[-2,-1,2,2,-2,1,2,-2],[1,-2,-1,-1,2,1,1,-2],[1,2,-2,2,2,2,1,1],[-2,1,-1,2,-2,-2,1,-1],[2,-2,-2,-2,-1,-1,-2,-1],[1,2,1,-1,2,-1,2,2],[1,-1,-2,2,-1,-1,1,-2],[-1,-1,-2,2,-2,2,2,1]]
CB = [[2,1],[2,1]]
def setup_inputs(rng):
    return {"x": rng.standard_normal((N, 128, TK), dtype=np.float32).astype(ml_dtypes.bfloat16), "a": (rng.standard_normal((N, 128, 128), dtype=np.float32) / 11).astype(ml_dtypes.bfloat16)}
def setup_inputs_big(rng):
    d = setup_inputs(rng)
    for k in ("x", "a"): d[k] = (d[k].astype(np.float32) * 1024.0).astype(d[k].dtype)
    return d
def setup_inputs_small(rng):
    d = setup_inputs(rng)
    for k in ("x", "a"): d[k] = (d[k].astype(np.float32) * (1 / 1024.0)).astype(d[k].dtype)
    return d
def setup_inputs_apart(rng):
    d = setup_inputs(rng)
    f = (10.0 ** rng.permutation(np.linspace(-1.5, 1.5, N))).astype(np.float32).reshape(N, 1, 1)
    for k in ("x", "a"): d[k] = (d[k].astype(np.float32) * f).astype(d[k].dtype)
    return d
def reference(x, a):
    X, A = x.astype(np.float64), a.astype(np.float64)
    y = np.zeros((N, 128, TK))
    for i in range(GR):
        for j in range(GC):
            t = sum(RA[i][k] * CB[j][l] * X[k * GC + l] for k in range(GR) for l in range(GC))
            y[i * GC + j] = A[i * GC + j].T @ t
    return {"y": y.astype(ml_dtypes.bfloat16)}

@@ -1,0 +1,241 @@
+from concourse.bass import DstId, RemoteDMATransfer
+from concourse.mybir import AluOpType
+
+TK = 512
+CHUNKS = [(0, 256, 0, False), (256, 512, 0, False)]
+NCH = len(CHUNKS)
+NLANES = 1 + max(ch[2] for ch in CHUNKS)
+
+SCRATCH = {
+    "xg": ("sbuf", [128, 4 * TK], "bfloat16"),
+    "asb": ("sbuf", [128, 128], "bfloat16"),
+    "wsb": ("sbuf", [128, TK], "bfloat16"),
+    "psb": ("sbuf", [128, TK], "bfloat16"),
+    "fin": ("sbuf", [128, 4 * TK], "bfloat16"),
+    "ysb": ("sbuf", [128, TK], "bfloat16"),
+    "idsrc": ("sbuf", [128, 129], "bfloat16"),
+    "iddram": ("dram", [129, 128], "bfloat16"),
+    "idm": ("sbuf", [128, 5 * 128], "bfloat16"),
+    "kc": ("sbuf", [128, 4 * 128], "bfloat16"),
+}
+for _c in range(NCH):
+    for _n in ("pw", "pp"):
+        SCRATCH["%s%d" % (_n, _c)] = ("psum", [128, 512], "float32")
+
+SEMAPHORES = ["lda", "ms", "mk", "id1", "id2", "idv", "ls"]
+for _c in range(NCH):
+    SEMAPHORES += ["%s%d" % (_n, _c) for _n in ("ld", "wd", "pd", "wc", "pc", "yd", "yc", "st", "fw0_", "fw1_", "fp_", "fo_",
+                                                "g0_", "g1_", "g2_", "g3_")]
+
+
+def _bits(m):
+    return bin(m).count("1")
+
+
+def _low(m, n):
+    out = 0
+    for b in range(m.bit_length()):
+        if (m >> b) & 1 and n > 0:
+            out |= 1 << b
+            n -= 1
+    return out
+
+
+def rank_program(g, core, T, topo):
+    S, cores = T.sem, T.cores
+    RA, CB = T.tables["RA"], T.tables["CB"]
+    GC, N = len(CB), len(cores)
+    assert all(row == CB[0] for row in CB)
+
+    def on_chip(a, b):
+        return topo.host(a) == topo.host(b) and topo.chip(a) == topo.chip(b)
+
+    owner = [q for q in range(N) if on_chip(cores[q], core)]
+    if not owner:
+        return
+    r = owner[0]
+
+    def coef(i, q):
+        return RA[i][q // GC] * CB[0][q % GC]
+
+    def partner(q):
+        return (q // GC) * GC + (GC - 1 - q % GC)
+
+    def peer(q):
+        c = cores[q]
+        p = [s for s in range(N) if topo.rack(topo.host(cores[s])) != topo.rack(topo.host(c))
+             and topo.may_write(c, cores[s]) and topo.chip(cores[s]) == topo.chip(c)]
+        assert len(p) == 1
+        return p[0]
+
+    def lanes(q):
+        rc = cores[q]
+        n = topo.CORES_PER_CHIP
+        need = [cores[peer(q)], cores[partner(peer(q))], cores[partner(q)]]
+        ok = [c for c in range(max(0, rc - n + 1), rc + n) if c != rc and on_chip(c, rc)
+              and all(topo.may_write(c, d) for d in need)]
+        ok.sort(key=lambda c: (topo.die(c) == topo.die(rc), c))
+        return [rc] + ok
+
+    mine = lanes(r)[:NLANES]
+    if core not in mine:
+        return
+    lane = mine.index(core)
+    rc = cores[r]
+
+    group = [q for q in range(N) if q == r or topo.same_plane(cores[q], rc)]
+    others = [q for q in group if q != r]
+    pos = group.index(r)
+    assert len(group) == 4 and partner(r) not in group
+    col = r % GC
+    w_dst = [peer(r), partner(peer(r))]
+    cw = {q: coef(peer(r) // GC, q) for q in group}
+    cp = {q: coef(r // GC, q) for q in group}
+    vals = sorted(set(list(cw.values()) + list(cp.values())) - {1})
+    assert len(vals) <= 4
+    ident = {1: T.idm[:, 0:128]}
+    for n, v in enumerate(vals):
+        ident[v] = T.idm[:, (n + 1) * 128:(n + 2) * 128]
+
+    m_off = topo.mask(core, cores[peer(r)])
+    for q in others + [partner(r), partner(peer(r))]:
+        m_off &= topo.mask(core, cores[q])
+    m_on_all = topo.mask(mine[0], mine[-1]) if NLANES > 1 else 0
+    m_on = m_on_all & ~m_off
+    N_OFF, N_ON4, N_ON8 = _bits(m_off), 4, 8
+
+    def xs(q, c):
+        o = group.index(q) * TK
+        return T.xg[:, o + CHUNKS[c][0]:o + CHUNKS[c][1]]
+
+    def tr(src, dst_ap, dst_cores, sem, m):
+        ids = []
+        for d in dst_cores:
+            rid, pid = topo.addr(d, core)
+            ids.append(DstId(rid=rid, pnc=pid))
+        return RemoteDMATransfer(dst_ids=ids, dma_engine_mask=m, remote_sem=sem, srcs=[src],
+                                 dsts=[dst_ap for _ in dst_cores], alu_op=0)
+
+    sent = [0]
+
+    def call(trs_masks):
+        g.remote_dma_fused([t for t, _ in trs_masks], local_sem=S.ls)
+        sent[0] += sum(_bits(m) for _, m in trs_masks)
+
+    V, TE = g.vector, g.tensor
+    dq = [g.sync, g.scalar]
+    my_chunks = [c for c in range(NCH) if CHUNKS[c][2] == lane]
+
+    if lane == 0:
+        for c, (c0, c1, ln, rl) in enumerate(CHUNKS):
+            dq[c % 2].dma_start(xs(r, c), T.x[:, c0:c1]).then_inc(S["ld%d" % c], 16)
+        g.scalar.dma_start(T.asb[:], T.a[:]).then_inc(S.lda, 16)
+
+    if my_chunks:
+        V.memset(T.idsrc[:, 1:129], 0.0).then_inc(S.ms, 1)
+        V.memset(T.idsrc[:, 0:1], 1.0).then_inc(S.ms, 1)
+        for n, v in enumerate(vals):
+            V.memset(T.kc[:, n * 128:(n + 1) * 128], float(v)).then_inc(S.mk, 1)
+        g.sync.wait_ge(S.ms, 2)
+        g.sync.dma_start(T.iddram[:], T.idsrc[:]).then_inc(S.id1, 16)
+        g.sync.wait_ge(S.id1, 16)
+        g.sync.dma_start(T.idm[:, 0:128], T.iddram[0:128, :]).then_inc(S.id2, 16)
+        V.wait_ge(S.mk, len(vals))
+        V.wait_ge(S.id2, 16)
+        for n, v in enumerate(vals):
+            V.tensor_tensor(out=ident[v], in0=T.idm[:, 0:128], in1=T.kc[:, n * 128:(n + 1) * 128],
+                            op=AluOpType.mult).then_inc(S.idv, 1)
+
+    def own_sem(c):
+        ln, rl = CHUNKS[c][2], CHUNKS[c][3]
+        if ln == 0:
+            return S["ld%d" % c], 16
+        return S["g%d_%d" % (pos, c)], (N_ON8 if rl else N_ON4)
+
+    for c, (c0, c1, ln, rl) in enumerate(CHUNKS):
+        sem = S["g%d_%d" % (pos, c)]
+        far = [lanes(q)[ln] for q in others]
+        if lane == 0:
+            g.wait_ge(S["ld%d" % c], 16)
+            if ln == 0:
+                call([(tr(xs(r, c), xs(r, c), far, sem, m_off), m_off)])
+            elif not rl:
+                m4 = _low(m_on, N_ON4)
+                call([(tr(xs(r, c), xs(r, c), far, sem, m_off), m_off),
+                      (tr(xs(r, c), xs(r, c), [mine[ln]], sem, m4), m4)])
+            else:
+                m8 = _low(m_on, N_ON8)
+                call([(tr(xs(r, c), xs(r, c), [mine[ln]], sem, m8), m8)])
+        elif lane == ln and rl:
+            g.wait_ge(sem, N_ON8)
+            call([(tr(xs(r, c), xs(r, c), far, sem, m_off), m_off)])
+
+    for c in my_chunks:
+        c0, c1 = CHUNKS[c][0], CHUNKS[c][1]
+        g.wait_ge(S["wc%d" % c], 1)
+        call([(tr(T.wsb[:, c0:c1], T.fin[:, col * TK + c0:col * TK + c1], [cores[d] for d in w_dst],
+                  S["fw%d_%d" % (col, c)], m_off), m_off)])
+        g.wait_ge(S["pc%d" % c], 1)
+        trs = [(tr(T.psb[:, c0:c1], T.fin[:, 2 * TK + c0:2 * TK + c1], [cores[partner(r)]], S["fp_%d" % c], m_off), m_off)]
+        if lane != 0:
+            m4 = _low(m_on, N_ON4)
+            trs.append((tr(T.psb[:, c0:c1], T.fin[:, 3 * TK + c0:3 * TK + c1], [rc], S["fo_%d" % c], m4), m4))
+        call(trs)
+    if sent[0]:
+        g.wait_ge(S.ls, sent[0])
+
+    if my_chunks:
+        TE.wait_ge(S.id2, 16)
+        TE.wait_ge(S.idv, len(vals))
+    for c in my_chunks:
+        w = CHUNKS[c][1] - CHUNKS[c][0]
+        sem, n = own_sem(c)
+        TE.wait_ge(sem, n)
+        TE.matmul(T["pw%d" % c][:, 0:w], ident[cw[r]], xs(r, c), start=True, stop=False)
+        TE.matmul(T["pp%d" % c][:, 0:w], ident[cp[r]], xs(r, c), start=True, stop=False)
+    for c in my_chunks:
+        w = CHUNKS[c][1] - CHUNKS[c][0]
+        for q in others:
+            TE.wait_ge(S["g%d_%d" % (group.index(q), c)], N_OFF)
+            mm = TE.matmul(T["pw%d" % c][:, 0:w], ident[cw[q]], xs(q, c), start=False, stop=(q == others[-1]))
+        mm.then_inc(S["wd%d" % c], 1)
+        for q in others:
+            mm = TE.matmul(T["pp%d" % c][:, 0:w], ident[cp[q]], xs(q, c), start=False, stop=(q == others[-1]))
+        mm.then_inc(S["pd%d" % c], 1)
+
+    for c in my_chunks:
+        c0, c1 = CHUNKS[c][0], CHUNKS[c][1]
+        w = c1 - c0
+        V.wait_ge(S["wd%d" % c], 1)
+        V.tensor_copy(out=T.wsb[:, c0:c1], in_=T["pw%d" % c][:, 0:w]).then_inc(S["wc%d" % c], 1)
+        V.wait_ge(S["pd%d" % c], 1)
+        V.tensor_copy(out=T.psb[:, c0:c1], in_=T["pp%d" % c][:, 0:w]).then_inc(S["pc%d" % c], 1)
+
+    if lane != 0:
+        return
+
+    TE.wait_ge(S.lda, 16)
+    for c, (c0, c1, ln, rl) in enumerate(CHUNKS):
+        w = c1 - c0
+        py = T["pw%d" % c][:, 0:w]
+        if ln == 0:
+            TE.wait_ge(S["wc%d" % c], 1)
+            TE.wait_ge(S["pc%d" % c], 1)
+            TE.matmul(py, T.asb[:], T.psb[:, c0:c1], start=True, stop=False)
+        else:
+            TE.wait_ge(S["fo_%d" % c], N_ON4)
+            TE.matmul(py, T.asb[:], T.fin[:, 3 * TK + c0:3 * TK + c1], start=True, stop=False)
+        for l in (col, GC - 1 - col):
+            TE.wait_ge(S["fw%d_%d" % (l, c)], N_OFF)
+            TE.matmul(py, T.asb[:], T.fin[:, l * TK + c0:l * TK + c1], start=False, stop=False)
+        TE.wait_ge(S["fp_%d" % c], N_OFF)
+        TE.matmul(py, T.asb[:], T.fin[:, 2 * TK + c0:2 * TK + c1], start=False, stop=True).then_inc(S["yd%d" % c], 1)
+
+    for c, (c0, c1, ln, rl) in enumerate(CHUNKS):
+        w = c1 - c0
+        V.wait_ge(S["yd%d" % c], 1)
+        V.tensor_copy(out=T.ysb[:, c0:c1], in_=T["pw%d" % c][:, 0:w]).then_inc(S["yc%d" % c], 1)
+        q = dq[c % 2]
+        q.wait_ge(S["yc%d" % c], 1)
+        q.dma_start(T.y[:, c0:c1], T.ysb[:, c0:c1]).then_inc(S["st%d" % c], 16)
+        q.wait_ge(S["st%d" % c], 16)

@@ -2,7 +2,7 @@ from concourse.bass import DstId, RemoteDMATransfer
 from concourse.mybir import AluOpType
 
 TK = 512
-CHUNKS = [(0, 256, 0, False), (256, 512, 0, False)]
+CHUNKS = [(256, 512, 1, False), (0, 256, 0, False)]
 NCH = len(CHUNKS)
 NLANES = 1 + max(ch[2] for ch in CHUNKS)
 

@@ -2,7 +2,7 @@ from concourse.bass import DstId, RemoteDMATransfer
 from concourse.mybir import AluOpType
 
 TK = 512
-CHUNKS = [(256, 512, 1, False), (0, 256, 0, False)]
+CHUNKS = [(256, 384, 1, False), (0, 128, 0, False), (384, 512, 1, False), (128, 256, 0, False)]
 NCH = len(CHUNKS)
 NLANES = 1 + max(ch[2] for ch in CHUNKS)
 

@@ -2,7 +2,7 @@ from concourse.bass import DstId, RemoteDMATransfer
 from concourse.mybir import AluOpType
 
 TK = 512
-CHUNKS = [(256, 384, 1, False), (0, 128, 0, False), (384, 512, 1, False), (128, 256, 0, False)]
+CHUNKS = [(256, 384, 1, False, True), (0, 128, 0, False, True), (384, 512, 1, True, False), (128, 256, 0, False, False)]
 NCH = len(CHUNKS)
 NLANES = 1 + max(ch[2] for ch in CHUNKS)
 
@@ -25,7 +25,7 @@ for _c in range(NCH):
 SEMAPHORES = ["lda", "ms", "mk", "id1", "id2", "idv", "ls"]
 for _c in range(NCH):
     SEMAPHORES += ["%s%d" % (_n, _c) for _n in ("ld", "wd", "pd", "wc", "pc", "yd", "yc", "st", "fw0_", "fw1_", "fp_", "fo_",
-                                                "g0_", "g1_", "g2_", "g3_")]
+                                                "fx_", "g0_", "g1_", "g2_", "g3_")]
 
 
 def _bits(m):
@@ -77,10 +77,15 @@ def rank_program(g, core, T, topo):
         ok.sort(key=lambda c: (topo.die(c) == topo.die(rc), c))
         return [rc] + ok
 
+    def fwd_core(q, ln):
+        L = lanes(q)
+        return [c for c in L[NLANES:] if topo.die(c) == topo.die(L[ln])][0]
+
     mine = lanes(r)[:NLANES]
-    if core not in mine:
+    fw_chunks = [c for c in range(NCH) if CHUNKS[c][4] and fwd_core(r, CHUNKS[c][2]) == core]
+    if core not in mine and not fw_chunks:
         return
-    lane = mine.index(core)
+    lane = mine.index(core) if core in mine else -1
     rc = cores[r]
 
     group = [q for q in range(N) if q == r or topo.same_plane(cores[q], rc)]
@@ -102,7 +107,7 @@ def rank_program(g, core, T, topo):
         m_off &= topo.mask(core, cores[q])
     m_on_all = topo.mask(mine[0], mine[-1]) if NLANES > 1 else 0
     m_on = m_on_all & ~m_off
-    N_OFF, N_ON4, N_ON8 = _bits(m_off), 4, 8
+    N_OFF, N_ON4, N_ON8 = _bits(m_off), 4, 4
 
     def xs(q, c):
         o = group.index(q) * TK
@@ -127,7 +132,7 @@ def rank_program(g, core, T, topo):
     my_chunks = [c for c in range(NCH) if CHUNKS[c][2] == lane]
 
     if lane == 0:
-        for c, (c0, c1, ln, rl) in enumerate(CHUNKS):
+        for c, (c0, c1, ln, rl, fw) in enumerate(CHUNKS):
             dq[c % 2].dma_start(xs(r, c), T.x[:, c0:c1]).then_inc(S["ld%d" % c], 16)
         g.scalar.dma_start(T.asb[:], T.a[:]).then_inc(S.lda, 16)
 
@@ -152,7 +157,7 @@ def rank_program(g, core, T, topo):
             return S["ld%d" % c], 16
         return S["g%d_%d" % (pos, c)], (N_ON8 if rl else N_ON4)
 
-    for c, (c0, c1, ln, rl) in enumerate(CHUNKS):
+    for c, (c0, c1, ln, rl, fw) in enumerate(CHUNKS):
         sem = S["g%d_%d" % (pos, c)]
         far = [lanes(q)[ln] for q in others]
         if lane == 0:
@@ -171,16 +176,27 @@ def rank_program(g, core, T, topo):
             call([(tr(xs(r, c), xs(r, c), far, sem, m_off), m_off)])
 
     for c in my_chunks:
-        c0, c1 = CHUNKS[c][0], CHUNKS[c][1]
+        c0, c1, fw = CHUNKS[c][0], CHUNKS[c][1], CHUNKS[c][4]
+        wl = T.fin[:, col * TK + c0:col * TK + c1]
         g.wait_ge(S["wc%d" % c], 1)
-        call([(tr(T.wsb[:, c0:c1], T.fin[:, col * TK + c0:col * TK + c1], [cores[d] for d in w_dst],
-                  S["fw%d_%d" % (col, c)], m_off), m_off)])
+        if fw:
+            call([(tr(T.wsb[:, c0:c1], wl, [fwd_core(peer(r), lane)], S["fx_%d" % c], m_off), m_off)])
+        else:
+            call([(tr(T.wsb[:, c0:c1], wl, [cores[d] for d in w_dst], S["fw%d_%d" % (col, c)], m_off), m_off)])
         g.wait_ge(S["pc%d" % c], 1)
         trs = [(tr(T.psb[:, c0:c1], T.fin[:, 2 * TK + c0:2 * TK + c1], [cores[partner(r)]], S["fp_%d" % c], m_off), m_off)]
         if lane != 0:
             m4 = _low(m_on, N_ON4)
             trs.append((tr(T.psb[:, c0:c1], T.fin[:, 3 * TK + c0:3 * TK + c1], [rc], S["fo_%d" % c], m4), m4))
         call(trs)
+
+    for c in fw_chunks:
+        c0, c1 = CHUNKS[c][0], CHUNKS[c][1]
+        wl = T.fin[:, col * TK + c0:col * TK + c1]
+        m4 = _low(m_on, N_ON4)
+        g.wait_ge(S["fx_%d" % c], N_OFF)
+        call([(tr(wl, wl, [cores[partner(r)]], S["fw%d_%d" % (col, c)], m_off), m_off),
+              (tr(wl, wl, [rc], S["fw%d_%d" % (col, c)], m4), m4)])
     if sent[0]:
         g.wait_ge(S.ls, sent[0])
 
@@ -215,7 +231,7 @@ def rank_program(g, core, T, topo):
         return
 
     TE.wait_ge(S.lda, 16)
-    for c, (c0, c1, ln, rl) in enumerate(CHUNKS):
+    for c, (c0, c1, ln, rl, fw) in enumerate(CHUNKS):
         w = c1 - c0
         py = T["pw%d" % c][:, 0:w]
         if ln == 0:
@@ -225,17 +241,19 @@ def rank_program(g, core, T, topo):
         else:
             TE.wait_ge(S["fo_%d" % c], N_ON4)
             TE.matmul(py, T.asb[:], T.fin[:, 3 * TK + c0:3 * TK + c1], start=True, stop=False)
-        for l in (col, GC - 1 - col):
-            TE.wait_ge(S["fw%d_%d" % (l, c)], N_OFF)
-            TE.matmul(py, T.asb[:], T.fin[:, l * TK + c0:l * TK + c1], start=False, stop=False)
         TE.wait_ge(S["fp_%d" % c], N_OFF)
-        TE.matmul(py, T.asb[:], T.fin[:, 2 * TK + c0:2 * TK + c1], start=False, stop=True).then_inc(S["yd%d" % c], 1)
+        TE.matmul(py, T.asb[:], T.fin[:, 2 * TK + c0:2 * TK + c1], start=False, stop=False)
+        for l in (col, GC - 1 - col):
+            TE.wait_ge(S["fw%d_%d" % (l, c)], N_ON4 if (fw and l == col) else N_OFF)
+            mm = TE.matmul(py, T.asb[:], T.fin[:, l * TK + c0:l * TK + c1], start=False, stop=(l != col))
+        mm.then_inc(S["yd%d" % c], 1)
 
-    for c, (c0, c1, ln, rl) in enumerate(CHUNKS):
+    for c, (c0, c1, ln, rl, fw) in enumerate(CHUNKS):
         w = c1 - c0
         V.wait_ge(S["yd%d" % c], 1)
         V.tensor_copy(out=T.ysb[:, c0:c1], in_=T["pw%d" % c][:, 0:w]).then_inc(S["yc%d" % c], 1)
         q = dq[c % 2]
         q.wait_ge(S["yc%d" % c], 1)
         q.dma_start(T.y[:, c0:c1], T.ysb[:, c0:c1]).then_inc(S["st%d" % c], 16)
-        q.wait_ge(S["st%d" % c], 16)
+    for c in range(NCH):
+        dq[c % 2].wait_ge(S["st%d" % c], 16)

@@ -2,9 +2,10 @@ from concourse.bass import DstId, RemoteDMATransfer
 from concourse.mybir import AluOpType
 
 TK = 512
-CHUNKS = [(256, 384, 1, False, True), (0, 128, 0, False, True), (384, 512, 1, True, False), (128, 256, 0, False, False)]
+CHUNKS = [(0, 136, 2, 1), (136, 272, 3, 1), (272, 376, 1, 0), (376, 512, 0, 0)]
 NCH = len(CHUNKS)
 NLANES = 1 + max(ch[2] for ch in CHUNKS)
+NID = 6
 
 SCRATCH = {
     "xg": ("sbuf", [128, 4 * TK], "bfloat16"),
@@ -13,19 +14,17 @@ SCRATCH = {
     "psb": ("sbuf", [128, TK], "bfloat16"),
     "fin": ("sbuf", [128, 4 * TK], "bfloat16"),
     "ysb": ("sbuf", [128, TK], "bfloat16"),
-    "idsrc": ("sbuf", [128, 129], "bfloat16"),
-    "iddram": ("dram", [129, 128], "bfloat16"),
-    "idm": ("sbuf", [128, 5 * 128], "bfloat16"),
-    "kc": ("sbuf", [128, 4 * 128], "bfloat16"),
+    "idm": ("sbuf", [128, NID * 128], "bfloat16"),
+    "kc": ("sbuf", [128, NID * 128], "bfloat16"),
 }
 for _c in range(NCH):
     for _n in ("pw", "pp"):
         SCRATCH["%s%d" % (_n, _c)] = ("psum", [128, 512], "float32")
 
-SEMAPHORES = ["lda", "ms", "mk", "id1", "id2", "idv", "ls"]
+SEMAPHORES = ["lda", "mk", "ia", "ls"] + ["it%d" % _l for _l in range(NID)]
 for _c in range(NCH):
     SEMAPHORES += ["%s%d" % (_n, _c) for _n in ("ld", "wd", "pd", "wc", "pc", "yd", "yc", "st", "fw0_", "fw1_", "fp_", "fo_",
-                                                "fx_", "g0_", "g1_", "g2_", "g3_")]
+                                                "g0_", "g1_", "g2_", "g3_")]
 
 
 def _bits(m):
@@ -61,56 +60,100 @@ def rank_program(g, core, T, topo):
     def partner(q):
         return (q // GC) * GC + (GC - 1 - q % GC)
 
-    def peer(q):
+    def rk(c):
+        return topo.rack(topo.host(c))
+
+    def hop(q, cable):
         c = cores[q]
-        p = [s for s in range(N) if topo.rack(topo.host(cores[s])) != topo.rack(topo.host(c))
-             and topo.may_write(c, cores[s]) and topo.chip(cores[s]) == topo.chip(c)]
+        p = [s for s in range(N) if topo.host(cores[s]) != topo.host(c) and topo.may_write(c, cores[s])
+             and topo.chip(cores[s]) == topo.chip(c) and (rk(cores[s]) != rk(c)) == cable]
         assert len(p) == 1
         return p[0]
+
+    def sib(q):
+        p = [s for s in range(N) if topo.host(cores[s]) == topo.host(cores[q]) and topo.same_plane(cores[s], cores[q])]
+        assert len(p) == 1
+        return p[0]
+
+    def near(q, plan):
+        return hop(q, plan == 1)
+
+    def far(q, plan):
+        return hop(q, plan == 0)
+
+    def grp(q, plan):
+        return sorted({q, sib(q), near(q, plan), near(sib(q), plan)})
 
     def lanes(q):
         rc = cores[q]
         n = topo.CORES_PER_CHIP
-        need = [cores[peer(q)], cores[partner(peer(q))], cores[partner(q)]]
+        need = [cores[partner(q)]]
+        for plan in (0, 1):
+            need += [cores[far(q, plan)], cores[partner(far(q, plan))]] + [cores[s] for s in grp(q, plan) if s != q]
         ok = [c for c in range(max(0, rc - n + 1), rc + n) if c != rc and on_chip(c, rc)
               and all(topo.may_write(c, d) for d in need)]
         ok.sort(key=lambda c: (topo.die(c) == topo.die(rc), c))
         return [rc] + ok
 
-    def fwd_core(q, ln):
-        L = lanes(q)
-        return [c for c in L[NLANES:] if topo.die(c) == topo.die(L[ln])][0]
-
     mine = lanes(r)[:NLANES]
-    fw_chunks = [c for c in range(NCH) if CHUNKS[c][4] and fwd_core(r, CHUNKS[c][2]) == core]
-    if core not in mine and not fw_chunks:
-        return
-    lane = mine.index(core) if core in mine else -1
+    assert len(mine) == NLANES
     rc = cores[r]
 
-    group = [q for q in range(N) if q == r or topo.same_plane(cores[q], rc)]
-    others = [q for q in group if q != r]
-    pos = group.index(r)
-    assert len(group) == 4 and partner(r) not in group
-    col = r % GC
-    w_dst = [peer(r), partner(peer(r))]
-    cw = {q: coef(peer(r) // GC, q) for q in group}
-    cp = {q: coef(r // GC, q) for q in group}
-    vals = sorted(set(list(cw.values()) + list(cp.values())) - {1})
-    assert len(vals) <= 4
-    ident = {1: T.idm[:, 0:128]}
-    for n, v in enumerate(vals):
-        ident[v] = T.idm[:, (n + 1) * 128:(n + 2) * 128]
+    def second(q, c):
+        d = near(sib(q), CHUNKS[c][3])
+        L = lanes(q)
+        n = topo.CORES_PER_CHIP
+        ok = [k for k in range(max(0, cores[q] - n + 1), cores[q] + n) if on_chip(k, cores[q]) and k not in L
+              and topo.die(k) == topo.die(L[CHUNKS[c][2]]) and topo.may_write(k, lanes(d)[CHUNKS[c][2]])]
+        return ok[0], d
 
-    m_off = topo.mask(core, cores[peer(r)])
-    for q in others + [partner(r), partner(peer(r))]:
-        m_off &= topo.mask(core, cores[q])
-    m_on_all = topo.mask(mine[0], mine[-1]) if NLANES > 1 else 0
-    m_on = m_on_all & ~m_off
-    N_OFF, N_ON4, N_ON8 = _bits(m_off), 4, 4
+    SEC = {c: second(r, c) for c in range(NCH) if CHUNKS[c][3] == 1}
+    sec_cores = [SEC[c][0] for c in sorted(SEC)]
+    if core not in mine and core not in sec_cores:
+        return
+    lane = mine.index(core) if core in mine else -1
+    for d in set(topo.die(c) for c in mine):
+        assert sorted(ch[3] for ch in CHUNKS if topo.die(mine[ch[2]]) == d) == [0, 1]
+
+    col = r % GC
+    G = [grp(r, ch[3]) for ch in CHUNKS]
+    POS = [G[c].index(r) for c in range(NCH)]
+    OTH = [sorted([q for q in G[c] if q != r], key=lambda q: (rk(cores[q]) != rk(rc), q)) for c in range(NCH)]
+    my_chunks = [c for c in range(NCH) if CHUNKS[c][2] == lane]
+    for c in range(NCH):
+        assert len(G[c]) == 4 and partner(r) not in G[c]
+    cw = {c: {q: coef(far(r, CHUNKS[c][3]) // GC, q) for q in G[c]} for c in range(NCH)}
+    cp = {c: {q: coef(r // GC, q) for q in G[c]} for c in range(NCH)}
+    need = [set() for _ in range(NLANES)]
+    for c in range(NCH):
+        need[CHUNKS[c][2]] |= set(cw[c].values()) | set(cp[c].values())
+    used = sorted(set().union(*need))
+    assert len(used) <= NID
+    ident = {v: T.idm[:, n * 128:(n + 1) * 128] for n, v in enumerate(used)}
+    HP = 64
+    NP = len(used) * (128 // HP)
+    BLD = mine + sec_cores
+    NB = len(BLD)
+    assert NB <= NID and NP >= NB
+    cnt = [NP // NB + (1 if b >= NB - NP % NB else 0) for b in range(NB)]
+    first = [sum(cnt[:b]) for b in range(NB)]
+    me = BLD.index(core)
+
+    def takers(b):
+        vs = set(used[p * HP // 128] for p in range(first[b], first[b] + cnt[b]))
+        return [k for k in range(NLANES) if mine[k] != BLD[b] and need[k] & vs]
+
+    m_all = topo.mask(core, [c for c in mine if c != core][0])
+    m_off = m_all
+    for q in range(N):
+        if q != r and topo.may_write(core, cores[q]):
+            m_off &= topo.mask(core, cores[q])
+    m_on = m_all & ~m_off
+    N_OFF, N_ON4 = _bits(m_off), 4
+    assert _bits(m_on) == N_OFF
 
     def xs(q, c):
-        o = group.index(q) * TK
+        o = G[c].index(q) * TK
         return T.xg[:, o + CHUNKS[c][0]:o + CHUNKS[c][1]]
 
     def tr(src, dst_ap, dst_cores, sem, m):
@@ -129,94 +172,89 @@ def rank_program(g, core, T, topo):
 
     V, TE = g.vector, g.tensor
     dq = [g.sync, g.scalar]
-    my_chunks = [c for c in range(NCH) if CHUNKS[c][2] == lane]
 
     if lane == 0:
-        for c, (c0, c1, ln, rl, fw) in enumerate(CHUNKS):
+        for c, (c0, c1, ln, plan) in enumerate(CHUNKS):
             dq[c % 2].dma_start(xs(r, c), T.x[:, c0:c1]).then_inc(S["ld%d" % c], 16)
         g.scalar.dma_start(T.asb[:], T.a[:]).then_inc(S.lda, 16)
 
-    if my_chunks:
-        V.memset(T.idsrc[:, 1:129], 0.0).then_inc(S.ms, 1)
-        V.memset(T.idsrc[:, 0:1], 1.0).then_inc(S.ms, 1)
-        for n, v in enumerate(vals):
-            V.memset(T.kc[:, n * 128:(n + 1) * 128], float(v)).then_inc(S.mk, 1)
-        g.sync.wait_ge(S.ms, 2)
-        g.sync.dma_start(T.iddram[:], T.idsrc[:]).then_inc(S.id1, 16)
-        g.sync.wait_ge(S.id1, 16)
-        g.sync.dma_start(T.idm[:, 0:128], T.iddram[0:128, :]).then_inc(S.id2, 16)
-        V.wait_ge(S.mk, len(vals))
-        V.wait_ge(S.id2, 16)
-        for n, v in enumerate(vals):
-            V.tensor_tensor(out=ident[v], in0=T.idm[:, 0:128], in1=T.kc[:, n * 128:(n + 1) * 128],
-                            op=AluOpType.mult).then_inc(S.idv, 1)
+    mp = range(first[me], first[me] + cnt[me])
+    for p in mp:
+        V.memset(T.kc[:, p * HP:(p + 1) * HP], float(used[p * HP // 128])).then_inc(S.mk, 1)
+    g.wait_ge(S.mk, cnt[me])
+    for p in mp:
+        g.affine_select(out=T.idm[:, p * HP:(p + 1) * HP], in_=T.kc[:, p * HP:(p + 1) * HP], pattern=[[-1, HP]],
+                        compare_op=AluOpType.is_equal, fill=0.0, base=-((p * HP) % 128),
+                        channel_multiplier=1).then_inc(S.ia, 1)
+    g.wait_ge(S.ia, cnt[me])
+    if takers(me):
+        share = T.idm[:, first[me] * HP:(first[me] + cnt[me]) * HP]
+        call([(tr(share, share, [mine[k] for k in takers(me)], S["it%d" % me], m_all), m_all)])
 
-    def own_sem(c):
-        ln, rl = CHUNKS[c][2], CHUNKS[c][3]
-        if ln == 0:
-            return S["ld%d" % c], 16
-        return S["g%d_%d" % (pos, c)], (N_ON8 if rl else N_ON4)
+    def gsem(c):
+        return S["g%d_%d" % (POS[c], c)]
 
-    for c, (c0, c1, ln, rl, fw) in enumerate(CHUNKS):
-        sem = S["g%d_%d" % (pos, c)]
-        far = [lanes(q)[ln] for q in others]
-        if lane == 0:
+    def step1(c, m, qs):
+        return (tr(xs(r, c), xs(r, c), [lanes(q)[CHUNKS[c][2]] for q in qs], gsem(c), m), m)
+
+    def hand(c, m):
+        return (tr(xs(r, c), xs(r, c), [mine[CHUNKS[c][2]]] + ([SEC[c][0]] if c in SEC else []), gsem(c), m), m)
+
+    if lane == 0:
+        ho = [c for c in range(NCH) if CHUNKS[c][2] != 0]
+        assert len(ho) == 3 and ho[0] in SEC and ho[1] in SEC
+        g.wait_ge(S["ld%d" % ho[0]], 16)
+        g.wait_ge(S["ld%d" % ho[1]], 16)
+        call([hand(ho[0], m_off), hand(ho[1], m_on)])
+        g.wait_ge(S["ld%d" % ho[2]], 16)
+        call([hand(ho[2], m_on)])
+        for c in my_chunks:
             g.wait_ge(S["ld%d" % c], 16)
-            if ln == 0:
-                call([(tr(xs(r, c), xs(r, c), far, sem, m_off), m_off)])
-            elif not rl:
-                m4 = _low(m_on, N_ON4)
-                call([(tr(xs(r, c), xs(r, c), far, sem, m_off), m_off),
-                      (tr(xs(r, c), xs(r, c), [mine[ln]], sem, m4), m4)])
-            else:
-                m8 = _low(m_on, N_ON8)
-                call([(tr(xs(r, c), xs(r, c), [mine[ln]], sem, m8), m8)])
-        elif lane == ln and rl:
-            g.wait_ge(sem, N_ON8)
-            call([(tr(xs(r, c), xs(r, c), far, sem, m_off), m_off)])
+            call([step1(c, m_off, OTH[c])])
+    elif lane > 0:
+        for c in my_chunks:
+            g.wait_ge(gsem(c), N_OFF)
+            call([step1(c, m_off, [q for q in OTH[c] if c not in SEC or q != SEC[c][1]])])
+    else:
+        for c in sorted(SEC):
+            if SEC[c][0] == core:
+                g.wait_ge(gsem(c), N_OFF)
+                call([step1(c, m_off, [SEC[c][1]])])
+        g.wait_ge(S.ls, sent[0])
+        return
 
     for c in my_chunks:
-        c0, c1, fw = CHUNKS[c][0], CHUNKS[c][1], CHUNKS[c][4]
-        wl = T.fin[:, col * TK + c0:col * TK + c1]
+        c0, c1, plan = CHUNKS[c][0], CHUNKS[c][1], CHUNKS[c][3]
+        f = far(r, plan)
         g.wait_ge(S["wc%d" % c], 1)
-        if fw:
-            call([(tr(T.wsb[:, c0:c1], wl, [fwd_core(peer(r), lane)], S["fx_%d" % c], m_off), m_off)])
-        else:
-            call([(tr(T.wsb[:, c0:c1], wl, [cores[d] for d in w_dst], S["fw%d_%d" % (col, c)], m_off), m_off)])
+        call([(tr(T.wsb[:, c0:c1], T.fin[:, col * TK + c0:col * TK + c1], [cores[f], cores[partner(f)]],
+                  S["fw%d_%d" % (col, c)], m_off), m_off)])
         g.wait_ge(S["pc%d" % c], 1)
         trs = [(tr(T.psb[:, c0:c1], T.fin[:, 2 * TK + c0:2 * TK + c1], [cores[partner(r)]], S["fp_%d" % c], m_off), m_off)]
         if lane != 0:
             m4 = _low(m_on, N_ON4)
             trs.append((tr(T.psb[:, c0:c1], T.fin[:, 3 * TK + c0:3 * TK + c1], [rc], S["fo_%d" % c], m4), m4))
         call(trs)
+    g.wait_ge(S.ls, sent[0])
 
-    for c in fw_chunks:
-        c0, c1 = CHUNKS[c][0], CHUNKS[c][1]
-        wl = T.fin[:, col * TK + c0:col * TK + c1]
-        m4 = _low(m_on, N_ON4)
-        g.wait_ge(S["fx_%d" % c], N_OFF)
-        call([(tr(wl, wl, [cores[partner(r)]], S["fw%d_%d" % (col, c)], m_off), m_off),
-              (tr(wl, wl, [rc], S["fw%d_%d" % (col, c)], m4), m4)])
-    if sent[0]:
-        g.wait_ge(S.ls, sent[0])
-
-    if my_chunks:
-        TE.wait_ge(S.id2, 16)
-        TE.wait_ge(S.idv, len(vals))
+    TE.wait_ge(S.ia, cnt[me])
+    for b in range(NB):
+        if lane in takers(b):
+            TE.wait_ge(S["it%d" % b], _bits(m_all))
     for c in my_chunks:
         w = CHUNKS[c][1] - CHUNKS[c][0]
-        sem, n = own_sem(c)
-        TE.wait_ge(sem, n)
-        TE.matmul(T["pw%d" % c][:, 0:w], ident[cw[r]], xs(r, c), start=True, stop=False)
-        TE.matmul(T["pp%d" % c][:, 0:w], ident[cp[r]], xs(r, c), start=True, stop=False)
-    for c in my_chunks:
-        w = CHUNKS[c][1] - CHUNKS[c][0]
-        for q in others:
-            TE.wait_ge(S["g%d_%d" % (group.index(q), c)], N_OFF)
-            mm = TE.matmul(T["pw%d" % c][:, 0:w], ident[cw[q]], xs(q, c), start=False, stop=(q == others[-1]))
+        if lane == 0:
+            TE.wait_ge(S["ld%d" % c], 16)
+        else:
+            TE.wait_ge(gsem(c), N_OFF)
+        TE.matmul(T["pw%d" % c][:, 0:w], ident[cw[c][r]], xs(r, c), start=True, stop=False)
+        TE.matmul(T["pp%d" % c][:, 0:w], ident[cp[c][r]], xs(r, c), start=True, stop=False)
+        for q in OTH[c]:
+            TE.wait_ge(S["g%d_%d" % (G[c].index(q), c)], N_OFF)
+            mm = TE.matmul(T["pw%d" % c][:, 0:w], ident[cw[c][q]], xs(q, c), start=False, stop=(q == OTH[c][-1]))
         mm.then_inc(S["wd%d" % c], 1)
-        for q in others:
-            mm = TE.matmul(T["pp%d" % c][:, 0:w], ident[cp[q]], xs(q, c), start=False, stop=(q == others[-1]))
+        for q in OTH[c]:
+            mm = TE.matmul(T["pp%d" % c][:, 0:w], ident[cp[c][q]], xs(q, c), start=False, stop=(q == OTH[c][-1]))
         mm.then_inc(S["pd%d" % c], 1)
 
     for c in my_chunks:
@@ -230,10 +268,11 @@ def rank_program(g, core, T, topo):
     if lane != 0:
         return
 
+    order = sorted(range(NCH), key=lambda c: CHUNKS[c][2])
     TE.wait_ge(S.lda, 16)
-    for c, (c0, c1, ln, rl, fw) in enumerate(CHUNKS):
-        w = c1 - c0
-        py = T["pw%d" % c][:, 0:w]
+    for c in order:
+        c0, c1, ln = CHUNKS[c][0], CHUNKS[c][1], CHUNKS[c][2]
+        py = T["pw%d" % c][:, 0:c1 - c0]
         if ln == 0:
             TE.wait_ge(S["wc%d" % c], 1)
             TE.wait_ge(S["pc%d" % c], 1)
@@ -241,19 +280,23 @@ def rank_program(g, core, T, topo):
         else:
             TE.wait_ge(S["fo_%d" % c], N_ON4)
             TE.matmul(py, T.asb[:], T.fin[:, 3 * TK + c0:3 * TK + c1], start=True, stop=False)
+    for l in (col, GC - 1 - col):
+        for c in order:
+            c0, c1 = CHUNKS[c][0], CHUNKS[c][1]
+            TE.wait_ge(S["fw%d_%d" % (l, c)], N_OFF)
+            TE.matmul(T["pw%d" % c][:, 0:c1 - c0], T.asb[:], T.fin[:, l * TK + c0:l * TK + c1], start=False, stop=False)
+    for c in order:
+        c0, c1 = CHUNKS[c][0], CHUNKS[c][1]
         TE.wait_ge(S["fp_%d" % c], N_OFF)
-        TE.matmul(py, T.asb[:], T.fin[:, 2 * TK + c0:2 * TK + c1], start=False, stop=False)
-        for l in (col, GC - 1 - col):
-            TE.wait_ge(S["fw%d_%d" % (l, c)], N_ON4 if (fw and l == col) else N_OFF)
-            mm = TE.matmul(py, T.asb[:], T.fin[:, l * TK + c0:l * TK + c1], start=False, stop=(l != col))
-        mm.then_inc(S["yd%d" % c], 1)
+        TE.matmul(T["pw%d" % c][:, 0:c1 - c0], T.asb[:], T.fin[:, 2 * TK + c0:2 * TK + c1], start=False,
+                  stop=True).then_inc(S["yd%d" % c], 1)
 
-    for c, (c0, c1, ln, rl, fw) in enumerate(CHUNKS):
-        w = c1 - c0
+    for n, c in enumerate(order):
+        c0, c1 = CHUNKS[c][0], CHUNKS[c][1]
         V.wait_ge(S["yd%d" % c], 1)
-        V.tensor_copy(out=T.ysb[:, c0:c1], in_=T["pw%d" % c][:, 0:w]).then_inc(S["yc%d" % c], 1)
-        q = dq[c % 2]
+        V.tensor_copy(out=T.ysb[:, c0:c1], in_=T["pw%d" % c][:, 0:c1 - c0]).then_inc(S["yc%d" % c], 1)
+        q = dq[n % 2]
         q.wait_ge(S["yc%d" % c], 1)
         q.dma_start(T.y[:, c0:c1], T.ysb[:, c0:c1]).then_inc(S["st%d" % c], 16)
-    for c in range(NCH):
-        dq[c % 2].wait_ge(S["st%d" % c], 16)
+    for n, c in enumerate(order):
+        dq[n % 2].wait_ge(S["st%d" % c], 16)

from concourse.bass import DstId, RemoteDMATransfer
from concourse.mybir import AluOpType

TK = 512
CHUNKS = [(0, 136, 2, 1), (136, 272, 3, 1), (272, 376, 1, 0), (376, 512, 0, 0)]
NCH = len(CHUNKS)
NLANES = 1 + max(ch[2] for ch in CHUNKS)
NID = 6

SCRATCH = {
    "xg": ("sbuf", [128, 4 * TK], "bfloat16"),
    "asb": ("sbuf", [128, 128], "bfloat16"),
    "wsb": ("sbuf", [128, TK], "bfloat16"),
    "psb": ("sbuf", [128, TK], "bfloat16"),
    "fin": ("sbuf", [128, 4 * TK], "bfloat16"),
    "ysb": ("sbuf", [128, TK], "bfloat16"),
    "idm": ("sbuf", [128, NID * 128], "bfloat16"),
    "kc": ("sbuf", [128, NID * 128], "bfloat16"),
}
for _c in range(NCH):
    for _n in ("pw", "pp"):
        SCRATCH["%s%d" % (_n, _c)] = ("psum", [128, 512], "float32")

SEMAPHORES = ["lda", "mk", "ia", "ls"] + ["it%d" % _l for _l in range(NID)]
for _c in range(NCH):
    SEMAPHORES += ["%s%d" % (_n, _c) for _n in ("ld", "wd", "pd", "wc", "pc", "yd", "yc", "st", "fw0_", "fw1_", "fp_", "fo_",
                                                "g0_", "g1_", "g2_", "g3_")]


def _bits(m):
    return bin(m).count("1")


def _low(m, n):
    out = 0
    for b in range(m.bit_length()):
        if (m >> b) & 1 and n > 0:
            out |= 1 << b
            n -= 1
    return out


def rank_program(g, core, T, topo):
    S, cores = T.sem, T.cores
    RA, CB = T.tables["RA"], T.tables["CB"]
    GC, N = len(CB), len(cores)
    assert all(row == CB[0] for row in CB)

    def on_chip(a, b):
        return topo.host(a) == topo.host(b) and topo.chip(a) == topo.chip(b)

    owner = [q for q in range(N) if on_chip(cores[q], core)]
    if not owner:
        return
    r = owner[0]

    def coef(i, q):
        return RA[i][q // GC] * CB[0][q % GC]

    def partner(q):
        return (q // GC) * GC + (GC - 1 - q % GC)

    def rk(c):
        return topo.rack(topo.host(c))

    def hop(q, cable):
        c = cores[q]
        p = [s for s in range(N) if topo.host(cores[s]) != topo.host(c) and topo.may_write(c, cores[s])
             and topo.chip(cores[s]) == topo.chip(c) and (rk(cores[s]) != rk(c)) == cable]
        assert len(p) == 1
        return p[0]

    def sib(q):
        p = [s for s in range(N) if topo.host(cores[s]) == topo.host(cores[q]) and topo.same_plane(cores[s], cores[q])]
        assert len(p) == 1
        return p[0]

    def near(q, plan):
        return hop(q, plan == 1)

    def far(q, plan):
        return hop(q, plan == 0)

    def grp(q, plan):
        return sorted({q, sib(q), near(q, plan), near(sib(q), plan)})

    def lanes(q):
        rc = cores[q]
        n = topo.CORES_PER_CHIP
        need = [cores[partner(q)]]
        for plan in (0, 1):
            need += [cores[far(q, plan)], cores[partner(far(q, plan))]] + [cores[s] for s in grp(q, plan) if s != q]
        ok = [c for c in range(max(0, rc - n + 1), rc + n) if c != rc and on_chip(c, rc)
              and all(topo.may_write(c, d) for d in need)]
        ok.sort(key=lambda c: (topo.die(c) == topo.die(rc), c))
        return [rc] + ok

    mine = lanes(r)[:NLANES]
    assert len(mine) == NLANES
    rc = cores[r]

    def second(q, c):
        d = near(sib(q), CHUNKS[c][3])
        L = lanes(q)
        n = topo.CORES_PER_CHIP
        ok = [k for k in range(max(0, cores[q] - n + 1), cores[q] + n) if on_chip(k, cores[q]) and k not in L
              and topo.die(k) == topo.die(L[CHUNKS[c][2]]) and topo.may_write(k, lanes(d)[CHUNKS[c][2]])]
        return ok[0], d

    SEC = {c: second(r, c) for c in range(NCH) if CHUNKS[c][3] == 1}
    sec_cores = [SEC[c][0] for c in sorted(SEC)]
    if core not in mine and core not in sec_cores:
        return
    lane = mine.index(core) if core in mine else -1
    for d in set(topo.die(c) for c in mine):
        assert sorted(ch[3] for ch in CHUNKS if topo.die(mine[ch[2]]) == d) == [0, 1]

    col = r % GC
    G = [grp(r, ch[3]) for ch in CHUNKS]
    POS = [G[c].index(r) for c in range(NCH)]
    OTH = [sorted([q for q in G[c] if q != r], key=lambda q: (rk(cores[q]) != rk(rc), q)) for c in range(NCH)]
    my_chunks = [c for c in range(NCH) if CHUNKS[c][2] == lane]
    for c in range(NCH):
        assert len(G[c]) == 4 and partner(r) not in G[c]
    cw = {c: {q: coef(far(r, CHUNKS[c][3]) // GC, q) for q in G[c]} for c in range(NCH)}
    cp = {c: {q: coef(r // GC, q) for q in G[c]} for c in range(NCH)}
    need = [set() for _ in range(NLANES)]
    for c in range(NCH):
        need[CHUNKS[c][2]] |= set(cw[c].values()) | set(cp[c].values())
    used = sorted(set().union(*need))
    assert len(used) <= NID
    ident = {v: T.idm[:, n * 128:(n + 1) * 128] for n, v in enumerate(used)}
    HP = 64
    NP = len(used) * (128 // HP)
    BLD = mine + sec_cores
    NB = len(BLD)
    assert NB <= NID and NP >= NB
    cnt = [NP // NB + (1 if b >= NB - NP % NB else 0) for b in range(NB)]
    first = [sum(cnt[:b]) for b in range(NB)]
    me = BLD.index(core)

    def takers(b):
        vs = set(used[p * HP // 128] for p in range(first[b], first[b] + cnt[b]))
        return [k for k in range(NLANES) if mine[k] != BLD[b] and need[k] & vs]

    m_all = topo.mask(core, [c for c in mine if c != core][0])
    m_off = m_all
    for q in range(N):
        if q != r and topo.may_write(core, cores[q]):
            m_off &= topo.mask(core, cores[q])
    m_on = m_all & ~m_off
    N_OFF, N_ON4 = _bits(m_off), 4
    assert _bits(m_on) == N_OFF

    def xs(q, c):
        o = G[c].index(q) * TK
        return T.xg[:, o + CHUNKS[c][0]:o + CHUNKS[c][1]]

    def tr(src, dst_ap, dst_cores, sem, m):
        ids = []
        for d in dst_cores:
            rid, pid = topo.addr(d, core)
            ids.append(DstId(rid=rid, pnc=pid))
        return RemoteDMATransfer(dst_ids=ids, dma_engine_mask=m, remote_sem=sem, srcs=[src],
                                 dsts=[dst_ap for _ in dst_cores], alu_op=0)

    sent = [0]

    def call(trs_masks):
        g.remote_dma_fused([t for t, _ in trs_masks], local_sem=S.ls)
        sent[0] += sum(_bits(m) for _, m in trs_masks)

    V, TE = g.vector, g.tensor
    dq = [g.sync, g.scalar]

    if lane == 0:
        for c, (c0, c1, ln, plan) in enumerate(CHUNKS):
            dq[c % 2].dma_start(xs(r, c), T.x[:, c0:c1]).then_inc(S["ld%d" % c], 16)
        g.scalar.dma_start(T.asb[:], T.a[:]).then_inc(S.lda, 16)

    mp = range(first[me], first[me] + cnt[me])
    for p in mp:
        V.memset(T.kc[:, p * HP:(p + 1) * HP], float(used[p * HP // 128])).then_inc(S.mk, 1)
    g.wait_ge(S.mk, cnt[me])
    for p in mp:
        g.affine_select(out=T.idm[:, p * HP:(p + 1) * HP], in_=T.kc[:, p * HP:(p + 1) * HP], pattern=[[-1, HP]],
                        compare_op=AluOpType.is_equal, fill=0.0, base=-((p * HP) % 128),
                        channel_multiplier=1).then_inc(S.ia, 1)
    g.wait_ge(S.ia, cnt[me])
    if takers(me):
        share = T.idm[:, first[me] * HP:(first[me] + cnt[me]) * HP]
        call([(tr(share, share, [mine[k] for k in takers(me)], S["it%d" % me], m_all), m_all)])

    def gsem(c):
        return S["g%d_%d" % (POS[c], c)]

    def step1(c, m, qs):
        return (tr(xs(r, c), xs(r, c), [lanes(q)[CHUNKS[c][2]] for q in qs], gsem(c), m), m)

    def hand(c, m):
        return (tr(xs(r, c), xs(r, c), [mine[CHUNKS[c][2]]] + ([SEC[c][0]] if c in SEC else []), gsem(c), m), m)

    if lane == 0:
        ho = [c for c in range(NCH) if CHUNKS[c][2] != 0]
        assert len(ho) == 3 and ho[0] in SEC and ho[1] in SEC
        g.wait_ge(S["ld%d" % ho[0]], 16)
        g.wait_ge(S["ld%d" % ho[1]], 16)
        call([hand(ho[0], m_off), hand(ho[1], m_on)])
        g.wait_ge(S["ld%d" % ho[2]], 16)
        call([hand(ho[2], m_on)])
        for c in my_chunks:
            g.wait_ge(S["ld%d" % c], 16)
            call([step1(c, m_off, OTH[c])])
    elif lane > 0:
        for c in my_chunks:
            g.wait_ge(gsem(c), N_OFF)
            call([step1(c, m_off, [q for q in OTH[c] if c not in SEC or q != SEC[c][1]])])
    else:
        for c in sorted(SEC):
            if SEC[c][0] == core:
                g.wait_ge(gsem(c), N_OFF)
                call([step1(c, m_off, [SEC[c][1]])])
        g.wait_ge(S.ls, sent[0])
        return

    for c in my_chunks:
        c0, c1, plan = CHUNKS[c][0], CHUNKS[c][1], CHUNKS[c][3]
        f = far(r, plan)
        g.wait_ge(S["wc%d" % c], 1)
        call([(tr(T.wsb[:, c0:c1], T.fin[:, col * TK + c0:col * TK + c1], [cores[f], cores[partner(f)]],
                  S["fw%d_%d" % (col, c)], m_off), m_off)])
        g.wait_ge(S["pc%d" % c], 1)
        trs = [(tr(T.psb[:, c0:c1], T.fin[:, 2 * TK + c0:2 * TK + c1], [cores[partner(r)]], S["fp_%d" % c], m_off), m_off)]
        if lane != 0:
            m4 = _low(m_on, N_ON4)
            trs.append((tr(T.psb[:, c0:c1], T.fin[:, 3 * TK + c0:3 * TK + c1], [rc], S["fo_%d" % c], m4), m4))
        call(trs)
    g.wait_ge(S.ls, sent[0])

    TE.wait_ge(S.ia, cnt[me])
    for b in range(NB):
        if lane in takers(b):
            TE.wait_ge(S["it%d" % b], _bits(m_all))
    for c in my_chunks:
        w = CHUNKS[c][1] - CHUNKS[c][0]
        if lane == 0:
            TE.wait_ge(S["ld%d" % c], 16)
        else:
            TE.wait_ge(gsem(c), N_OFF)
        TE.matmul(T["pw%d" % c][:, 0:w], ident[cw[c][r]], xs(r, c), start=True, stop=False)
        TE.matmul(T["pp%d" % c][:, 0:w], ident[cp[c][r]], xs(r, c), start=True, stop=False)
        for q in OTH[c]:
            TE.wait_ge(S["g%d_%d" % (G[c].index(q), c)], N_OFF)
            mm = TE.matmul(T["pw%d" % c][:, 0:w], ident[cw[c][q]], xs(q, c), start=False, stop=(q == OTH[c][-1]))
        mm.then_inc(S["wd%d" % c], 1)
        for q in OTH[c]:
            mm = TE.matmul(T["pp%d" % c][:, 0:w], ident[cp[c][q]], xs(q, c), start=False, stop=(q == OTH[c][-1]))
        mm.then_inc(S["pd%d" % c], 1)

    for c in my_chunks:
        c0, c1 = CHUNKS[c][0], CHUNKS[c][1]
        w = c1 - c0
        V.wait_ge(S["wd%d" % c], 1)
        V.tensor_copy(out=T.wsb[:, c0:c1], in_=T["pw%d" % c][:, 0:w]).then_inc(S["wc%d" % c], 1)
        V.wait_ge(S["pd%d" % c], 1)
        V.tensor_copy(out=T.psb[:, c0:c1], in_=T["pp%d" % c][:, 0:w]).then_inc(S["pc%d" % c], 1)

    if lane != 0:
        return

    order = sorted(range(NCH), key=lambda c: CHUNKS[c][2])
    TE.wait_ge(S.lda, 16)
    for c in order:
        c0, c1, ln = CHUNKS[c][0], CHUNKS[c][1], CHUNKS[c][2]
        py = T["pw%d" % c][:, 0:c1 - c0]
        if ln == 0:
            TE.wait_ge(S["wc%d" % c], 1)
            TE.wait_ge(S["pc%d" % c], 1)
            TE.matmul(py, T.asb[:], T.psb[:, c0:c1], start=True, stop=False)
        else:
            TE.wait_ge(S["fo_%d" % c], N_ON4)
            TE.matmul(py, T.asb[:], T.fin[:, 3 * TK + c0:3 * TK + c1], start=True, stop=False)
    for l in (col, GC - 1 - col):
        for c in order:
            c0, c1 = CHUNKS[c][0], CHUNKS[c][1]
            TE.wait_ge(S["fw%d_%d" % (l, c)], N_OFF)
            TE.matmul(T["pw%d" % c][:, 0:c1 - c0], T.asb[:], T.fin[:, l * TK + c0:l * TK + c1], start=False, stop=False)
    for c in order:
        c0, c1 = CHUNKS[c][0], CHUNKS[c][1]
        TE.wait_ge(S["fp_%d" % c], N_OFF)
        TE.matmul(T["pw%d" % c][:, 0:c1 - c0], T.asb[:], T.fin[:, 2 * TK + c0:2 * TK + c1], start=False,
                  stop=True).then_inc(S["yd%d" % c], 1)

    for n, c in enumerate(order):
        c0, c1 = CHUNKS[c][0], CHUNKS[c][1]
        V.wait_ge(S["yd%d" % c], 1)
        V.tensor_copy(out=T.ysb[:, c0:c1], in_=T["pw%d" % c][:, 0:c1 - c0]).then_inc(S["yc%d" % c], 1)
        q = dq[n % 2]
        q.wait_ge(S["yc%d" % c], 1)
        q.dma_start(T.y[:, c0:c1], T.ysb[:, c0:c1]).then_inc(S["st%d" % c], 16)
    for n, c in enumerate(order):
        dq[n % 2].wait_ge(S["st%d" % c], 16)
